import numpy as np
import ml_dtypes


def mxq(x, axis, fmt="e4m3"):
    dtype, down = {"e4m3": (ml_dtypes.float8_e4m3fn, 7), "e5m2": (ml_dtypes.float8_e5m2, 14)}[fmt]
    v = np.moveaxis(np.asarray(x, np.float32).astype(ml_dtypes.bfloat16).astype(np.float64), axis, -1)
    blocks = v.reshape(v.shape[:-1] + (-1, 32))
    amax = np.abs(blocks).max(-1, keepdims=True)
    byte = np.maximum(np.where(amax > 0, np.frexp(amax)[1] - 1 + 127, 0) - down, 1)
    scale = np.exp2(byte - 127.0)
    codes = (blocks / scale).astype(np.float32).astype(dtype).astype(np.float64)
    return np.moveaxis((codes * scale).reshape(v.shape), -1, axis)


WIDE = False


def mx_kscale(k):
    if not WIDE:
        return np.ones(k)
    levels = np.array([10, -10, 5, -5, 0])
    if k % 512:
        return np.exp2(np.random.permutation(np.resize(levels, k // 32))).repeat(32)
    a = np.empty((k // 512, 16))
    for p in range(k // 512):
        a[p, :8] = np.random.permutation(np.resize(levels, 8))
        for g in range(8):
            far = levels[np.abs(levels - a[p, g]) >= 10]
            a[p, g + 8] = far[np.random.randint(len(far))]
    return np.exp2(a.ravel()).repeat(32)


def f64(x):
    return np.asarray(x).astype(np.float64)


def striped(idx):
    return np.tile(idx.reshape(-1, 16).T, (8, 1)).astype(np.uint16)


def unstriped(offs):
    return offs[:16].T.reshape(-1).astype(np.int64)


E2M1 = np.array([0.0, 0.5, 1.0, 1.5, 2.0, 3.0, 4.0, 6.0, -0.0, -0.5, -1.0, -1.5, -2.0, -3.0, -4.0, -6.0])


def pack_weight(w, fmt):
    k, n = w.shape
    w = f64(np.asarray(w, np.float32).astype(ml_dtypes.bfloat16)).reshape(k // 32, 32, n)
    amax = np.abs(w).max(1)
    if fmt == "e4m3":
        byte = np.frexp(amax)[1] - 1 + 127 - 7
    else:
        mant, ex = np.frexp(amax / 6.0)
        byte = np.where(mant > 0.5, ex, ex - 1) + 127
    byte = np.clip(np.where(amax > 0, byte, 1), 1, 254)
    scaled = (w * np.exp2(127.0 - byte)[:, None, :]).reshape(k, n).astype(np.float32)
    by_word = np.ascontiguousarray(scaled.reshape(k // 512, 128, 4, n).transpose(0, 1, 3, 2))
    if fmt == "e4m3":
        words = by_word.astype(ml_dtypes.float8_e4m3fn).view(np.uint8)
    else:
        c = by_word.astype(ml_dtypes.float4_e2m1fn).view(np.uint8) & 0xF
        words = (c[..., 0::2] | (c[..., 1::2] << 4)).reshape(k // 512, 128, 2 * n)
    return np.ascontiguousarray(words), np.ascontiguousarray(byte.astype(np.uint8).reshape(k // 512, 16, n))


def unpack_weight(words, scales, fmt):
    g, _, n = scales.shape
    words = np.ascontiguousarray(words).reshape(g, 128, n, -1)
    if fmt == "e4m3":
        vals = words.view(ml_dtypes.float8_e4m3fn).astype(np.float64)
    else:
        nib = np.empty((g, 128, n, 4), np.uint8)
        nib[..., 0::2] = words & 0xF
        nib[..., 1::2] = words >> 4
        vals = E2M1[nib]
    vals = vals * np.repeat(np.exp2(scales.astype(np.float64) - 127.0), 8, axis=1)[..., None]
    return vals.transpose(0, 1, 3, 2).reshape(g * 512, n)


def gelu(v):
    return 0.5 * v * (1.0 + np.tanh(np.sqrt(2.0 / np.pi) * (v + 0.044715 * v**3)))


K, H, N, T, S = 1024, 512, 768, 2048, 1024


def setup_inputs():
    n = np.random.standard_normal
    s = mx_kscale(K)[:, None]
    u = mx_kscale(H)[:, None]
    tab_words, tab_scales = pack_weight(n((K, T)) * s, "e4m3")
    w2_words, w2_scales = pack_weight(1.3 * n((H, H)) / np.sqrt(H) / u, "e2m1")
    return {
        "tab_words": tab_words,
        "tab_scales": tab_scales,
        "offs": striped(np.random.permutation(T)[:S]),
        "offs2": striped(np.random.permutation(S)),
        "w1": (n((K, H)) / np.sqrt(K) / s).astype(np.float32),
        "ga": (np.exp(0.2 * n(H)) * u[:, 0]).astype(np.float32),
        "w2_words": w2_words,
        "w2_scales": w2_scales,
        "gb": (np.exp(0.2 * n(H)) * u[:, 0]).astype(np.float32),
        "w3": (n((H, N)) / np.sqrt(H) / u).astype(np.float32),
        "wgo": np.exp(0.3 * n((128, S))).astype(np.float32),
        "x0": n((N, S)).astype(np.float32),
    }


def reference(tab_words, tab_scales, offs, offs2, w1, ga, w2_words, w2_scales, gb, w3, wgo, x0):
    v = unpack_weight(tab_words, tab_scales, "e4m3")[:, unstriped(offs)]
    a = mxq(f64(w1), 0, "e4m3").T @ v
    gelu = 0.5 * a * (1.0 + np.tanh(np.sqrt(2.0 / np.pi) * (a + 0.044715 * a * a * a)))
    h = f64(ga)[:, None] * gelu
    w2 = unpack_weight(w2_words, w2_scales, "e2m1")
    b = w2.T @ mxq(h, 0, "e4m3")
    z = h + f64(gb)[:, None] * np.tanh(b)
    y = mxq(f64(w3), 0, "e4m3").T @ mxq(z, 0, "e4m3")
    page = np.zeros((N, S))
    page[:, unstriped(offs2)] = np.tile(f64(wgo), (N // 128, 1)) * y
    return page * f64(x0)

@@ -1,0 +1,271 @@
+from contextlib import ExitStack
+
+import concourse.mybir as mybir
+
+K, H, N, T, S = 1024, 512, 768, 2048, 1024
+FLOPS = 2 * S * (K * H + H * H + H * N)
+
+F32 = mybir.dt.float32
+BF16 = mybir.dt.bfloat16
+I32 = mybir.dt.int32
+U32 = mybir.dt.uint32
+U16 = mybir.dt.uint16
+U8 = mybir.dt.uint8
+FP8X4 = mybir.dt.float8_e4m3fn_x4
+FP4X4 = mybir.dt.float4_e2m1fn_x4
+MULT = mybir.AluOpType.mult
+ADD = mybir.AluOpType.add
+ACT = mybir.ActivationFunctionType
+
+P = 128
+PACK = 4
+BANK = 512
+PER_COL = 16
+PASSES = K // (P * PACK)
+ROW_TILES = N // P
+W3_PIECE = 256
+CHUNK = 256
+CHUNKS = S // CHUNK
+PAIR = BANK // CHUNK
+VECTOR_CHUNKS = 1
+
+
+def tile_list_jury_rank_cascade_kernel(
+    tc, tab_words, tab_scales, offs, offs2, w1, ga, w2_words, w2_scales, gb, w3, wgo, x0, out
+):
+    nc = tc.nc
+    with ExitStack() as ctx:
+        keep = ctx.enter_context(tc.tile_pool(name="keep", bufs=1))
+        psum = ctx.enter_context(tc.psum_pool(name="psum", bufs=1))
+
+        def tile(name, shape, dtype):
+            return keep.tile(shape, dtype, name=name, align_bytes=64)
+
+        picks = keep.tile([P, S // PER_COL], U16, name="picks")
+        places = keep.tile([P, S // PER_COL], U16, name="places")
+        table = [tile("table%d" % a, [P, T], I32) for a in range(PASSES)]
+        table_scale = tile("table_scale", [P, T], U8)
+        w1_raw = [tile("w1_raw%d" % a, [P, PACK, H], F32) for a in range(PASSES)]
+        w3_raw = [tile("w3_raw%d" % i, [P, PACK, W3_PIECE], F32) for i in range(N // W3_PIECE)]
+        wgo_sb = tile("wgo_sb", [P, S], F32)
+        x0_sb = [tile("x0_sb%d" % n, [P, S], F32) for n in range(ROW_TILES)]
+        w2_raw = tile("w2_raw", [P, 2 * H], U8)
+        w2_raw_scale = tile("w2_raw_scale", [P, H], U8)
+        ga_sb = tile("ga_sb", [P, PACK], F32)
+        gb_sb = tile("gb_sb", [P, PACK], F32)
+
+        nc.vector.memset(table_scale[:].bitcast(I32), 0)
+        zero_in = tile("zero_in", [P, 1], F32)
+        zero = tile("zero", [P, 1], F32)
+        nc.vector.memset(zero_in[:], 0.0)
+        nc.scalar.activation(zero[:], zero_in[:], ACT.Gelu_apprx_tanh)
+
+        def load_table(a):
+            nc.sync.dma_start(table[a][:], tab_words[a].rearrange("p t i -> p (t i)").bitcast(I32))
+
+        def load_w1(a):
+            rows = w1[a * P * PACK : (a + 1) * P * PACK, :]
+            nc.sync.dma_start(w1_raw[a][:], rows.rearrange("(p j) c -> p j c", j=PACK))
+
+        def load_w3(i):
+            cols = w3[:, i * W3_PIECE : (i + 1) * W3_PIECE]
+            nc.sync.dma_start(w3_raw[i][:], cols.rearrange("(p j) c -> p j c", j=PACK))
+
+        nc.gpsimd.memset(w2_raw_scale[:].bitcast(I32), 0)
+        nc.gpsimd.dma_start(ga_sb[:], ga.rearrange("(p t) -> p t", t=PACK))
+        nc.gpsimd.dma_start(gb_sb[:], gb.rearrange("(p t) -> p t", t=PACK))
+
+        load_table(0)
+        nc.sync.dma_start(picks[:], offs)
+        for q in range(4):
+            nc.sync.dma_start(
+                table_scale[32 * q : 32 * q + 4 * PASSES, :].bitcast(I32),
+                tab_scales.bitcast(I32)[:, 4 * q : 4 * q + 4, :],
+            )
+        load_w1(0)
+        load_w1(1)
+        load_table(1)
+        nc.sync.dma_start(w2_raw[:].bitcast(I32), w2_words[0].bitcast(I32))
+        for q in range(4):
+            nc.sync.dma_start(
+                w2_raw_scale[32 * q : 32 * q + 4, :].bitcast(I32),
+                w2_scales[0].bitcast(I32)[4 * q : 4 * q + 4, :],
+            )
+        load_w3(0)
+        nc.sync.dma_start(wgo_sb[:], wgo)
+        nc.sync.dma_start(places[:], offs2)
+        load_w3(1)
+        load_w3(2)
+        for n in range(ROW_TILES):
+            nc.sync.dma_start(x0_sb[n][:], x0[n * P : (n + 1) * P, :])
+
+        picked_early = tile("picked_early", [P, S], U32)
+        picked_late = tile("picked_late", [P, CHUNK], U32)
+        picked_scale = tile("picked_scale", [P, S], U8)
+
+        def gather_late(c):
+            lo = c * CHUNK // PER_COL
+            window = table[1][:].bitcast(U32).indirect(picks[:, lo : lo + CHUNK // PER_COL])
+            nc.vector.tensor_copy(picked_late[:], window)
+
+        nc.vector.tensor_copy(picked_early[:], table[0][:].bitcast(U32).indirect(picks[:]))
+        nc.vector.tensor_copy(picked_scale[:], table_scale[:].indirect(picks[:]))
+
+        def quantize(codes, scale, grouped):
+            nc.vector.quantize_mx(out=codes.bitcast(FP8X4), scales=scale, in_=grouped)
+
+        w1_codes = [tile("w1_codes%d" % a, [P, H], U32) for a in range(PASSES)]
+        w1_scale = [tile("w1_scale%d" % a, [P, H], U8) for a in range(PASSES)]
+        w1_grouped = [tile("w1_grouped%d" % a, [P, PACK * H], BF16) for a in range(PASSES)]
+
+        def group_w1(copy, a, lo, hi):
+            dst = w1_grouped[a][:].rearrange("p (t m j) -> p m j t", t=PACK, j=PACK)
+            src = w1_raw[a][:].rearrange("p j (m t) -> p m j t", t=PACK)
+            copy(dst[:, lo:hi], src[:, lo:hi])
+
+        group_w1(nc.scalar.copy, 0, 0, P)
+        group_w1(nc.vector.tensor_copy, 1, 0, P // 2)
+        quantize(w1_codes[0][:], w1_scale[0][:], w1_grouped[0][:])
+        group_w1(nc.scalar.copy, 1, P // 2, P)
+        quantize(w1_codes[1][:], w1_scale[1][:], w1_grouped[1][:])
+        gather_late(0)
+
+        w2_codes = tile("w2_codes", [P, 2 * H], U8)
+        w2_scale = tile("w2_scale", [P, H], U8)
+        nc.vector.tensor_copy(
+            w2_codes[:].bitcast(U16).rearrange("p (t m) -> p t m", t=PACK),
+            w2_raw[:].bitcast(U16).rearrange("p (m t) -> p t m", t=PACK),
+        )
+        nc.vector.tensor_copy(
+            w2_scale[:].rearrange("p (t m) -> p t m", t=PACK),
+            w2_raw_scale[:].rearrange("p (m t) -> p t m", t=PACK),
+        )
+
+        def interleave(copy, grouped, planes):
+            copy(
+                grouped.rearrange("p (c i t) -> p c t i", i=4, t=PACK),
+                planes.rearrange("p t (c i) -> p c t i", i=4),
+            )
+
+        w3_codes = tile("w3_codes", [P, N], U32)
+        w3_scale = tile("w3_scale", [P, N], U8)
+
+        def prepare_w3(i):
+            grouped = tile("w3_grouped%d" % i, [P, PACK * W3_PIECE], BF16)
+            interleave(nc.scalar.copy, grouped[:], w3_raw[i][:])
+            cols = slice(i * W3_PIECE, (i + 1) * W3_PIECE)
+            quantize(w3_codes[:, cols], w3_scale[:, cols], grouped[:])
+
+        banks_a = [psum.tile([P, PAIR, CHUNK], F32, name="bank_a%d" % i) for i in range(2)]
+        banks_b = [psum.tile([P, PAIR, CHUNK], F32, name="bank_b%d" % i) for i in range(2)]
+        banks_y = [psum.tile([P, PAIR, CHUNK], F32, name="bank_y%d" % i) for i in range(3)]
+
+        gelu = tile("gelu", [P, PACK, CHUNK], F32)
+        h = [tile("h%d" % i, [P, PACK, CHUNK], F32) for i in range(2)]
+        h_grouped = tile("h_grouped", [P, PACK * CHUNK], BF16)
+        h_codes = tile("h_codes", [P, CHUNK], U32)
+        h_scale = tile("h_scale", [P, CHUNK], U8)
+        bent = tile("bent", [P, PACK, CHUNK], F32)
+        z = tile("z", [P, PACK, CHUNK], F32)
+        z_grouped = tile("z_grouped", [P, PACK * CHUNK], BF16)
+        z_codes = [tile("z_codes%d" % i, [P, CHUNK], U32) for i in range(2)]
+        z_scale = [tile("z_scale%d" % i, [P, CHUNK], U8) for i in range(2)]
+        y = [tile("y%d" % i, [P, PAIR, CHUNK], F32) for i in range(3)]
+        page = [tile("page%d" % n, [P, S], F32) for n in range(ROW_TILES)]
+
+        def mover(c):
+            return nc.vector.tensor_copy if c < VECTOR_CHUNKS else nc.scalar.copy
+
+        def make_h(c):
+            cols = slice(c * CHUNK, (c + 1) * CHUNK)
+            moving = (picked_early[:, cols], picked_late[:])
+            for i, bank in enumerate(banks_a):
+                for u in range(PAIR):
+                    ch = slice((PAIR * i + u) * P, (PAIR * i + u + 1) * P)
+                    for a in range(PASSES):
+                        nc.tensor.matmul_mx(
+                            out=bank[:, u, :],
+                            lhsT=w1_codes[a][:, ch].bitcast(FP8X4),
+                            lhsT_scale=w1_scale[a][:, ch],
+                            rhs=moving[a].bitcast(FP8X4),
+                            rhs_scale=picked_scale[4 * a : P, cols],
+                            start=(a == 0),
+                            stop=(a == PASSES - 1),
+                        )
+                nc.scalar.activation(gelu[:, PAIR * i : PAIR * (i + 1), :], bank[:], ACT.Gelu_apprx_tanh, bias=zero[:])
+                for t in range(PAIR * i, PAIR * (i + 1)):
+                    if c < VECTOR_CHUNKS:
+                        nc.vector.tensor_scalar(h[c % 2][:, t, :], gelu[:, t, :], ga_sb[:, t : t + 1], None, MULT)
+                    else:
+                        nc.scalar.activation(h[c % 2][:, t, :], gelu[:, t, :], ACT.Copy, scale=ga_sb[:, t : t + 1])
+            if c + 1 < CHUNKS:
+                gather_late(c + 1)
+            interleave(mover(c), h_grouped[:], h[c % 2][:])
+            quantize(h_codes[:], h_scale[:], h_grouped[:])
+
+        def make_z(c):
+            for i, bank in enumerate(banks_b):
+                for u in range(PAIR):
+                    t = PAIR * i + u
+                    nc.tensor.matmul_mx(
+                        out=bank[:, u, :],
+                        lhsT=w2_codes[:, 2 * t * P : 2 * (t + 1) * P].bitcast(FP4X4),
+                        lhsT_scale=w2_scale[:, t * P : (t + 1) * P],
+                        rhs=h_codes[:].bitcast(FP8X4),
+                        rhs_scale=h_scale[:],
+                        start=True,
+                        stop=True,
+                    )
+                nc.scalar.activation(bent[:, PAIR * i : PAIR * (i + 1), :], bank[:], ACT.Tanh, bias=zero[:])
+                for t in range(PAIR * i, PAIR * (i + 1)):
+                    nc.vector.scalar_tensor_tensor(
+                        z[:, t, :], bent[:, t, :], gb_sb[:, t : t + 1], h[c % 2][:, t, :], MULT, ADD
+                    )
+
+        def quantize_z(c):
+            interleave(mover(c), z_grouped[:], z[:])
+            quantize(z_codes[c % 2][:], z_scale[c % 2][:], z_grouped[:])
+
+        def finish(n, lo, hi):
+            nc.vector.tensor_tensor(x0_sb[n][:, lo:hi], page[n][:, lo:hi], x0_sb[n][:, lo:hi], MULT)
+            nc.sync.dma_start(out[n * P : (n + 1) * P, lo:hi], x0_sb[n][:, lo:hi])
+
+        def put_back(c, i, bank, staged):
+            cols = slice(c * CHUNK, (c + 1) * CHUNK)
+            for u in range(PAIR):
+                rows = slice((PAIR * i + u) * P, (PAIR * i + u + 1) * P)
+                nc.tensor.matmul_mx(
+                    out=bank[:, u, :],
+                    lhsT=w3_codes[:, rows].bitcast(FP8X4),
+                    lhsT_scale=w3_scale[:, rows],
+                    rhs=z_codes[c % 2][:].bitcast(FP8X4),
+                    rhs_scale=z_scale[c % 2][:],
+                    start=True,
+                    stop=True,
+                )
+            nc.scalar.copy(staged, bank[:])
+            for u in range(PAIR):
+                n = PAIR * i + u
+                window = page[n][:].indirect(places[:, cols.start // PER_COL : cols.stop // PER_COL])
+                nc.vector.tensor_tensor(window, staged[:, u, :], wgo_sb[:, cols], MULT)
+                if c == CHUNKS - 1 and n > 0:
+                    finish(n - 1, 0, S)
+
+        make_h(0)
+        prepare_w3(0)
+        make_z(0)
+        quantize_z(0)
+        for c in range(CHUNKS - 1):
+            make_h(c + 1)
+            put_back(c, 0, banks_y[0], y[0][:])
+            if c == 0:
+                prepare_w3(1)
+                prepare_w3(2)
+            make_z(c + 1)
+            put_back(c, 1, banks_b[0], y[1][:])
+            quantize_z(c + 1)
+            put_back(c, 2, banks_y[1], z[:, 0:PAIR, :])
+        for i in range(ROW_TILES // PAIR):
+            put_back(CHUNKS - 1, i, banks_y[(i + 2) % 3], y[(i + 2) % 3][:])
+        finish(ROW_TILES - 1, 0, S // 2)
+        finish(ROW_TILES - 1, S // 2, S)

@@ -54,7 +54,7 @@ def tile_list_jury_rank_cascade_kernel(
         ga_sb = tile("ga_sb", [P, PACK], F32)
         gb_sb = tile("gb_sb", [P, PACK], F32)
 
-        nc.vector.memset(table_scale[:].bitcast(I32), 0)
+        nc.gpsimd.memset(table_scale[:].bitcast(I32), 0)
         zero_in = tile("zero_in", [P, 1], F32)
         zero = tile("zero", [P, 1], F32)
         nc.vector.memset(zero_in[:], 0.0)
@@ -158,7 +158,7 @@ def tile_list_jury_rank_cascade_kernel(
 
         banks_a = [psum.tile([P, PAIR, CHUNK], F32, name="bank_a%d" % i) for i in range(2)]
         banks_b = [psum.tile([P, PAIR, CHUNK], F32, name="bank_b%d" % i) for i in range(2)]
-        banks_y = [psum.tile([P, PAIR, CHUNK], F32, name="bank_y%d" % i) for i in range(3)]
+        banks_y = [psum.tile([P, PAIR, CHUNK], F32, name="bank_y%d" % i) for i in range(4)]
 
         gelu = tile("gelu", [P, PACK, CHUNK], F32)
         h = [tile("h%d" % i, [P, PACK, CHUNK], F32) for i in range(2)]
@@ -168,8 +168,8 @@ def tile_list_jury_rank_cascade_kernel(
         bent = tile("bent", [P, PACK, CHUNK], F32)
         z = tile("z", [P, PACK, CHUNK], F32)
         z_grouped = tile("z_grouped", [P, PACK * CHUNK], BF16)
-        z_codes = [tile("z_codes%d" % i, [P, CHUNK], U32) for i in range(2)]
-        z_scale = [tile("z_scale%d" % i, [P, CHUNK], U8) for i in range(2)]
+        z_codes = tile("z_codes", [P, S], U32)
+        z_scale = tile("z_scale", [P, S], U8)
         y = [tile("y%d" % i, [P, PAIR, CHUNK], F32) for i in range(3)]
         page = [tile("page%d" % n, [P, S], F32) for n in range(ROW_TILES)]
 
@@ -224,32 +224,53 @@ def tile_list_jury_rank_cascade_kernel(
 
         def quantize_z(c):
             interleave(mover(c), z_grouped[:], z[:])
-            quantize(z_codes[c % 2][:], z_scale[c % 2][:], z_grouped[:])
-
-        def finish(n, lo, hi):
-            nc.vector.tensor_tensor(x0_sb[n][:, lo:hi], page[n][:, lo:hi], x0_sb[n][:, lo:hi], MULT)
-            nc.sync.dma_start(out[n * P : (n + 1) * P, lo:hi], x0_sb[n][:, lo:hi])
-
-        def put_back(c, i, bank, staged):
             cols = slice(c * CHUNK, (c + 1) * CHUNK)
-            for u in range(PAIR):
-                rows = slice((PAIR * i + u) * P, (PAIR * i + u + 1) * P)
-                nc.tensor.matmul_mx(
-                    out=bank[:, u, :],
-                    lhsT=w3_codes[:, rows].bitcast(FP8X4),
-                    lhsT_scale=w3_scale[:, rows],
-                    rhs=z_codes[c % 2][:].bitcast(FP8X4),
-                    rhs_scale=z_scale[c % 2][:],
-                    start=True,
-                    stop=True,
-                )
-            nc.scalar.copy(staged, bank[:])
-            for u in range(PAIR):
-                n = PAIR * i + u
-                window = page[n][:].indirect(places[:, cols.start // PER_COL : cols.stop // PER_COL])
-                nc.vector.tensor_tensor(window, staged[:, u, :], wgo_sb[:, cols], MULT)
-                if c == CHUNKS - 1 and n > 0:
-                    finish(n - 1, 0, S)
+            quantize(z_codes[:, cols], z_scale[:, cols], z_grouped[:])
+
+        def flat(pair):
+            return pair.rearrange("p u c -> p (u c)")
+
+        def product(n, cols, acc):
+            rows = slice(n * P, (n + 1) * P)
+            nc.tensor.matmul_mx(
+                out=acc,
+                lhsT=w3_codes[:, rows].bitcast(FP8X4),
+                lhsT_scale=w3_scale[:, rows],
+                rhs=z_codes[:, cols].bitcast(FP8X4),
+                rhs_scale=z_scale[:, cols],
+                start=True,
+                stop=True,
+            )
+
+        def window(n, cols):
+            return page[n][:].indirect(places[:, cols.start // PER_COL : cols.stop // PER_COL])
+
+        def stage_chunk(c, first, count, bank, staged):
+            cols = slice(c * CHUNK, (c + 1) * CHUNK)
+            for u in range(count):
+                product(first + u, cols, bank[:, u, :])
+            nc.scalar.copy(staged[:, 0:count, :], bank[:, 0:count, :])
+
+        def put_back(c, first, count, bank, staged):
+            cols = slice(c * CHUNK, (c + 1) * CHUNK)
+            stage_chunk(c, first, count, bank, staged)
+            for u in range(count):
+                nc.vector.tensor_tensor(window(first + u, cols), staged[:, u, :], wgo_sb[:, cols], MULT)
+
+        def weigh(values, cols):
+            nc.gpsimd.tensor_tensor(values, values, wgo_sb[:, cols], MULT)
+
+        def stage_half(n, cols, bank, staged):
+            product(n, cols, flat(bank[:]))
+            nc.scalar.copy(staged, flat(bank[:]))
+            weigh(staged, cols)
+
+        def scatter(n, cols, values):
+            nc.vector.tensor_copy(window(n, cols), values)
+
+        def finish(engine, n, lo, hi):
+            engine.tensor_tensor(x0_sb[n][:, lo:hi], page[n][:, lo:hi], x0_sb[n][:, lo:hi], MULT)
+            nc.sync.dma_start(out[n * P : (n + 1) * P, lo:hi], x0_sb[n][:, lo:hi])
 
         make_h(0)
         prepare_w3(0)
@@ -257,15 +278,36 @@ def tile_list_jury_rank_cascade_kernel(
         quantize_z(0)
         for c in range(CHUNKS - 1):
             make_h(c + 1)
-            put_back(c, 0, banks_y[0], y[0][:])
+            put_back(c, 0, 1, banks_y[0], y[0])
             if c == 0:
                 prepare_w3(1)
-                prepare_w3(2)
             make_z(c + 1)
-            put_back(c, 1, banks_b[0], y[1][:])
+            put_back(c, 1, 2, banks_b[0], y[1])
             quantize_z(c + 1)
-            put_back(c, 2, banks_y[1], z[:, 0:PAIR, :])
-        for i in range(ROW_TILES // PAIR):
-            put_back(CHUNKS - 1, i, banks_y[(i + 2) % 3], y[(i + 2) % 3][:])
-        finish(ROW_TILES - 1, 0, S // 2)
-        finish(ROW_TILES - 1, S // 2, S)
+            put_back(c, 3, 1, banks_y[1], z)
+        prepare_w3(2)
+
+        low, high = slice(0, S // 2), slice(S // 2, S)
+        last = slice(S - CHUNK, S)
+        spare = flat(z[:, 2:4, :])
+        product(4, low, flat(banks_y[2][:]))
+        nc.vector.tensor_tensor(spare, flat(banks_y[2][:]), wgo_sb[:, low], MULT)
+        scatter(4, low, spare)
+        for i in range(2):
+            stage_chunk(CHUNKS - 1, PAIR * i, PAIR, banks_y[i], y[i])
+            for u in range(PAIR):
+                weigh(y[i][:, u, :], last)
+        stage_half(4, high, banks_y[3], flat(y[2][:]))
+        stage_half(5, low, banks_y[2], spare)
+        for n in range(4):
+            scatter(n, last, y[n // PAIR][:, n % PAIR, :])
+            if n < 3:
+                finish(nc.gpsimd, n, 0, S)
+        stage_half(5, high, banks_b[1], flat(y[0][:]))
+        scatter(4, high, flat(y[2][:]))
+        finish(nc.gpsimd, 3, 0, S)
+        scatter(5, low, spare)
+        finish(nc.gpsimd, 4, 0, S)
+        scatter(5, high, flat(y[0][:]))
+        finish(nc.vector, 5, 0, S // 2)
+        finish(nc.vector, 5, S // 2, S)

@@ -24,10 +24,11 @@ PER_COL = 16
 PASSES = K // (P * PACK)
 ROW_TILES = N // P
 W3_PIECE = 256
-CHUNK = 256
-CHUNKS = S // CHUNK
-PAIR = BANK // CHUNK
-VECTOR_CHUNKS = 1
+WIDTHS = (256, 256, 256, 256)
+WIDE = 256
+FUSED = 2
+VZB = 1
+VW3 = 2
 
 
 def tile_list_jury_rank_cascade_kernel(
@@ -45,7 +46,8 @@ def tile_list_jury_rank_cascade_kernel(
         places = keep.tile([P, S // PER_COL], U16, name="places")
         table = [tile("table%d" % a, [P, T], I32) for a in range(PASSES)]
         table_scale = tile("table_scale", [P, T], U8)
-        w1_raw = [tile("w1_raw%d" % a, [P, PACK, H], F32) for a in range(PASSES)]
+        w1_early = tile("w1_early", [P, PACK, H], F32)
+        w1_late = [tile("w1_late%d" % i, [P, PACK, H // 2], F32) for i in range(2)]
         w3_raw = [tile("w3_raw%d" % i, [P, PACK, W3_PIECE], F32) for i in range(N // W3_PIECE)]
         wgo_sb = tile("wgo_sb", [P, S], F32)
         x0_sb = [tile("x0_sb%d" % n, [P, S], F32) for n in range(ROW_TILES)]
@@ -63,9 +65,9 @@ def tile_list_jury_rank_cascade_kernel(
         def load_table(a):
             nc.sync.dma_start(table[a][:], tab_words[a].rearrange("p t i -> p (t i)").bitcast(I32))
 
-        def load_w1(a):
-            rows = w1[a * P * PACK : (a + 1) * P * PACK, :]
-            nc.sync.dma_start(w1_raw[a][:], rows.rearrange("(p j) c -> p j c", j=PACK))
+        def load_w1(raw, a, cols):
+            rows = w1[a * P * PACK : (a + 1) * P * PACK, cols]
+            nc.sync.dma_start(raw[:], rows.rearrange("(p j) c -> p j c", j=PACK))
 
         def load_w3(i):
             cols = w3[:, i * W3_PIECE : (i + 1) * W3_PIECE]
@@ -75,41 +77,37 @@ def tile_list_jury_rank_cascade_kernel(
         nc.gpsimd.dma_start(ga_sb[:], ga.rearrange("(p t) -> p t", t=PACK))
         nc.gpsimd.dma_start(gb_sb[:], gb.rearrange("(p t) -> p t", t=PACK))
 
-        load_table(0)
         nc.sync.dma_start(picks[:], offs)
+        nc.sync.dma_start(w2_raw[:].bitcast(I32), w2_words[0].bitcast(I32))
+        nc.sync.dma_start(places[:], offs2)
         for q in range(4):
             nc.sync.dma_start(
                 table_scale[32 * q : 32 * q + 4 * PASSES, :].bitcast(I32),
                 tab_scales.bitcast(I32)[:, 4 * q : 4 * q + 4, :],
             )
-        load_w1(0)
-        load_w1(1)
+        load_table(0)
         load_table(1)
-        nc.sync.dma_start(w2_raw[:].bitcast(I32), w2_words[0].bitcast(I32))
+        load_w1(w1_early, 0, slice(0, H))
         for q in range(4):
             nc.sync.dma_start(
                 w2_raw_scale[32 * q : 32 * q + 4, :].bitcast(I32),
                 w2_scales[0].bitcast(I32)[4 * q : 4 * q + 4, :],
             )
+        for i in range(2):
+            load_w1(w1_late[i], 1, slice(i * H // 2, (i + 1) * H // 2))
         load_w3(0)
         nc.sync.dma_start(wgo_sb[:], wgo)
-        nc.sync.dma_start(places[:], offs2)
         load_w3(1)
         load_w3(2)
         for n in range(ROW_TILES):
             nc.sync.dma_start(x0_sb[n][:], x0[n * P : (n + 1) * P, :])
 
-        picked_early = tile("picked_early", [P, S], U32)
-        picked_late = tile("picked_late", [P, CHUNK], U32)
+        picked = [tile("picked%d" % a, [P, S], U32) for a in range(PASSES)]
         picked_scale = tile("picked_scale", [P, S], U8)
 
-        def gather_late(c):
-            lo = c * CHUNK // PER_COL
-            window = table[1][:].bitcast(U32).indirect(picks[:, lo : lo + CHUNK // PER_COL])
-            nc.vector.tensor_copy(picked_late[:], window)
-
-        nc.vector.tensor_copy(picked_early[:], table[0][:].bitcast(U32).indirect(picks[:]))
         nc.vector.tensor_copy(picked_scale[:], table_scale[:].indirect(picks[:]))
+        for a in range(PASSES):
+            nc.vector.tensor_copy(picked[a][:], table[a][:].bitcast(U32).indirect(picks[:]))
 
         def quantize(codes, scale, grouped):
             nc.vector.quantize_mx(out=codes.bitcast(FP8X4), scales=scale, in_=grouped)
@@ -118,17 +116,18 @@ def tile_list_jury_rank_cascade_kernel(
         w1_scale = [tile("w1_scale%d" % a, [P, H], U8) for a in range(PASSES)]
         w1_grouped = [tile("w1_grouped%d" % a, [P, PACK * H], BF16) for a in range(PASSES)]
 
-        def group_w1(copy, a, lo, hi):
+        def group_w1(copy, a, half, raw):
             dst = w1_grouped[a][:].rearrange("p (t m j) -> p m j t", t=PACK, j=PACK)
-            src = w1_raw[a][:].rearrange("p j (m t) -> p m j t", t=PACK)
-            copy(dst[:, lo:hi], src[:, lo:hi])
+            copy(dst[:, half * P // 2 : (half + 1) * P // 2], raw.rearrange("p j (m t) -> p m j t", t=PACK))
 
-        group_w1(nc.scalar.copy, 0, 0, P)
-        group_w1(nc.vector.tensor_copy, 1, 0, P // 2)
+        group_w1(nc.scalar.copy, 0, 0, w1_early[:, :, 0 : H // 2])
+        group_w1(nc.vector.tensor_copy, 0, 1, w1_early[:, :, H // 2 : H])
         quantize(w1_codes[0][:], w1_scale[0][:], w1_grouped[0][:])
-        group_w1(nc.scalar.copy, 1, P // 2, P)
-        quantize(w1_codes[1][:], w1_scale[1][:], w1_grouped[1][:])
-        gather_late(0)
+        group_w1(nc.scalar.copy, 1, 0, w1_late[0][:])
+        group_w1(nc.vector.tensor_copy, 1, 1, w1_late[1][:])
+        for lo in (0, H // 2):
+            cols = slice(lo, lo + H // 2)
+            quantize(w1_codes[1][:, cols], w1_scale[1][:, cols], w1_grouped[1][:, PACK * cols.start : PACK * cols.stop])
 
         w2_codes = tile("w2_codes", [P, 2 * H], U8)
         w2_scale = tile("w2_scale", [P, H], U8)
@@ -150,87 +149,112 @@ def tile_list_jury_rank_cascade_kernel(
         w3_codes = tile("w3_codes", [P, N], U32)
         w3_scale = tile("w3_scale", [P, N], U8)
 
-        def prepare_w3(i):
-            grouped = tile("w3_grouped%d" % i, [P, PACK * W3_PIECE], BF16)
-            interleave(nc.scalar.copy, grouped[:], w3_raw[i][:])
+        def prepare_w3(i, grouped):
+            interleave(nc.vector.tensor_copy if i < VW3 else nc.scalar.copy, grouped[:], w3_raw[i][:])
             cols = slice(i * W3_PIECE, (i + 1) * W3_PIECE)
             quantize(w3_codes[:, cols], w3_scale[:, cols], grouped[:])
 
-        banks_a = [psum.tile([P, PAIR, CHUNK], F32, name="bank_a%d" % i) for i in range(2)]
-        banks_b = [psum.tile([P, PAIR, CHUNK], F32, name="bank_b%d" % i) for i in range(2)]
-        banks_y = [psum.tile([P, PAIR, CHUNK], F32, name="bank_y%d" % i) for i in range(4)]
+        banks = [psum.tile([P, BANK], F32, name="bank%d" % i) for i in range(8)]
+        banks_a, banks_b, banks_y = banks[0:2], banks[2:4], banks[4:8]
 
-        gelu = tile("gelu", [P, PACK, CHUNK], F32)
-        h = [tile("h%d" % i, [P, PACK, CHUNK], F32) for i in range(2)]
-        h_grouped = tile("h_grouped", [P, PACK * CHUNK], BF16)
-        h_codes = tile("h_codes", [P, CHUNK], U32)
-        h_scale = tile("h_scale", [P, CHUNK], U8)
-        bent = tile("bent", [P, PACK, CHUNK], F32)
-        z = tile("z", [P, PACK, CHUNK], F32)
-        z_grouped = tile("z_grouped", [P, PACK * CHUNK], BF16)
+        gelus = [tile("gelu%d" % i, [P, PACK * WIDE], F32) for i in range(2)]
+        h = [tile("h%d" % i, [P, PACK * WIDE], F32) for i in range(2)]
+        h_grouped = tile("h_grouped", [P, PACK * WIDE], BF16)
+        h_codes = tile("h_codes", [P, WIDE], U32)
+        h_scale = tile("h_scale", [P, WIDE], U8)
+        bent = tile("bent", [P, PACK * WIDE], F32)
+        z = tile("z", [P, PACK * WIDE], F32)
+        z_grouped = tile("z_grouped", [P, PACK * WIDE], BF16)
         z_codes = tile("z_codes", [P, S], U32)
         z_scale = tile("z_scale", [P, S], U8)
-        y = [tile("y%d" % i, [P, PAIR, CHUNK], F32) for i in range(3)]
+        y = [tile("y%d" % i, [P, BANK], F32) for i in range(3)]
         page = [tile("page%d" % n, [P, S], F32) for n in range(ROW_TILES)]
 
-        def mover(c):
-            return nc.vector.tensor_copy if c < VECTOR_CHUNKS else nc.scalar.copy
+        def columns(c):
+            return slice(sum(WIDTHS[:c]), sum(WIDTHS[: c + 1]))
+
+        def planes(flat, width):
+            return flat[:, 0 : PACK * width].rearrange("p (t c) -> p t c", t=PACK)
+
+        def first_product(c, t, acc):
+            cols = columns(c)
+            ch = slice(t * P, (t + 1) * P)
+            for a in range(PASSES):
+                nc.tensor.matmul_mx(
+                    out=acc,
+                    lhsT=w1_codes[a][:, ch].bitcast(FP8X4),
+                    lhsT_scale=w1_scale[a][:, ch],
+                    rhs=picked[a][:, cols].bitcast(FP8X4),
+                    rhs_scale=picked_scale[4 * a : P, cols],
+                    start=(a == 0),
+                    stop=(a == PASSES - 1),
+                )
+
+        def second_product(c, t, acc):
+            width = WIDTHS[c]
+            nc.tensor.matmul_mx(
+                out=acc,
+                lhsT=w2_codes[:, 2 * t * P : 2 * (t + 1) * P].bitcast(FP4X4),
+                lhsT_scale=w2_scale[:, t * P : (t + 1) * P],
+                rhs=h_codes[:, 0:width].bitcast(FP8X4),
+                rhs_scale=h_scale[:, 0:width],
+                start=True,
+                stop=True,
+            )
+
+        def activate(c, product, func, dst, used, after):
+            width = WIDTHS[c]
+            share = PACK // len(used)
+            for i, bank in enumerate(used):
+                for u in range(share):
+                    product(c, share * i + u, bank[:, u * width : (u + 1) * width])
+                span = slice(share * i * width, share * (i + 1) * width)
+                nc.scalar.activation(dst[:, span], bank[:, 0 : share * width], func, bias=zero[:])
+                for t in range(share * i, share * (i + 1)):
+                    after(t, slice(t * width, (t + 1) * width))
+
+        def quantize_h(c):
+            width = WIDTHS[c]
+            quantize(h_codes[:, 0:width], h_scale[:, 0:width], h_grouped[:, 0 : PACK * width])
+
+        def gain(c, t, plane):
+            nc.scalar.activation(h[c % 2][:, plane], gelus[min(c, 1)][:, plane], ACT.Copy, scale=ga_sb[:, t : t + 1])
+
+        def make_h_fused(c, used):
+            width = WIDTHS[c]
+            activate(c, first_product, ACT.Gelu_apprx_tanh, gelus[min(c, 1)], used, lambda t, plane: None)
+            gains = ga_sb[:].unsqueeze(1).unsqueeze(3).to_broadcast([P, width // 4, PACK, 4])
+            nc.vector.tensor_tensor(
+                h_grouped[:, 0 : PACK * width].rearrange("p (c i t) -> p c t i", i=4, t=PACK),
+                planes(gelus[min(c, 1)], width).rearrange("p t (c i) -> p c t i", i=4),
+                gains,
+                MULT,
+            )
+            quantize_h(c)
+            for t in range(PACK):
+                gain(c, t, slice(t * width, (t + 1) * width))
 
         def make_h(c):
-            cols = slice(c * CHUNK, (c + 1) * CHUNK)
-            moving = (picked_early[:, cols], picked_late[:])
-            for i, bank in enumerate(banks_a):
-                for u in range(PAIR):
-                    ch = slice((PAIR * i + u) * P, (PAIR * i + u + 1) * P)
-                    for a in range(PASSES):
-                        nc.tensor.matmul_mx(
-                            out=bank[:, u, :],
-                            lhsT=w1_codes[a][:, ch].bitcast(FP8X4),
-                            lhsT_scale=w1_scale[a][:, ch],
-                            rhs=moving[a].bitcast(FP8X4),
-                            rhs_scale=picked_scale[4 * a : P, cols],
-                            start=(a == 0),
-                            stop=(a == PASSES - 1),
-                        )
-                nc.scalar.activation(gelu[:, PAIR * i : PAIR * (i + 1), :], bank[:], ACT.Gelu_apprx_tanh, bias=zero[:])
-                for t in range(PAIR * i, PAIR * (i + 1)):
-                    if c < VECTOR_CHUNKS:
-                        nc.vector.tensor_scalar(h[c % 2][:, t, :], gelu[:, t, :], ga_sb[:, t : t + 1], None, MULT)
-                    else:
-                        nc.scalar.activation(h[c % 2][:, t, :], gelu[:, t, :], ACT.Copy, scale=ga_sb[:, t : t + 1])
-            if c + 1 < CHUNKS:
-                gather_late(c + 1)
-            interleave(mover(c), h_grouped[:], h[c % 2][:])
-            quantize(h_codes[:], h_scale[:], h_grouped[:])
+            width = WIDTHS[c]
+            activate(c, first_product, ACT.Gelu_apprx_tanh, gelus[min(c, 1)], banks_a, lambda t, plane: gain(c, t, plane))
+            interleave(nc.scalar.copy, h_grouped[:, 0 : PACK * width], planes(h[c % 2], width))
+            quantize_h(c)
 
-        def make_z(c):
-            for i, bank in enumerate(banks_b):
-                for u in range(PAIR):
-                    t = PAIR * i + u
-                    nc.tensor.matmul_mx(
-                        out=bank[:, u, :],
-                        lhsT=w2_codes[:, 2 * t * P : 2 * (t + 1) * P].bitcast(FP4X4),
-                        lhsT_scale=w2_scale[:, t * P : (t + 1) * P],
-                        rhs=h_codes[:].bitcast(FP8X4),
-                        rhs_scale=h_scale[:],
-                        start=True,
-                        stop=True,
-                    )
-                nc.scalar.activation(bent[:, PAIR * i : PAIR * (i + 1), :], bank[:], ACT.Tanh, bias=zero[:])
-                for t in range(PAIR * i, PAIR * (i + 1)):
-                    nc.vector.scalar_tensor_tensor(
-                        z[:, t, :], bent[:, t, :], gb_sb[:, t : t + 1], h[c % 2][:, t, :], MULT, ADD
-                    )
+        def make_z(c, used):
+            def add(t, plane):
+                nc.vector.scalar_tensor_tensor(
+                    z[:, plane], bent[:, plane], gb_sb[:, t : t + 1], h[c % 2][:, plane], MULT, ADD
+                )
 
-        def quantize_z(c):
-            interleave(mover(c), z_grouped[:], z[:])
-            cols = slice(c * CHUNK, (c + 1) * CHUNK)
-            quantize(z_codes[:, cols], z_scale[:, cols], z_grouped[:])
+            activate(c, second_product, ACT.Tanh, bent, used, add)
 
-        def flat(pair):
-            return pair.rearrange("p u c -> p (u c)")
+        def quantize_z(c, copy):
+            width = WIDTHS[c]
+            cols = columns(c)
+            interleave(copy, z_grouped[:, 0 : PACK * width], planes(z, width))
+            quantize(z_codes[:, cols], z_scale[:, cols], z_grouped[:, 0 : PACK * width])
 
-        def product(n, cols, acc):
+        def third_product(n, cols, acc):
             rows = slice(n * P, (n + 1) * P)
             nc.tensor.matmul_mx(
                 out=acc,
@@ -245,69 +269,75 @@ def tile_list_jury_rank_cascade_kernel(
         def window(n, cols):
             return page[n][:].indirect(places[:, cols.start // PER_COL : cols.stop // PER_COL])
 
-        def stage_chunk(c, first, count, bank, staged):
-            cols = slice(c * CHUNK, (c + 1) * CHUNK)
-            for u in range(count):
-                product(first + u, cols, bank[:, u, :])
-            nc.scalar.copy(staged[:, 0:count, :], bank[:, 0:count, :])
+        def stage(pieces, bank, staged):
+            spans = []
+            used = 0
+            for n, cols in pieces:
+                spans.append(slice(used, used + cols.stop - cols.start))
+                third_product(n, cols, bank[:, spans[-1]])
+                used = spans[-1].stop
+            nc.scalar.copy(staged[:, 0:used], bank[:, 0:used])
+            return spans
 
-        def put_back(c, first, count, bank, staged):
-            cols = slice(c * CHUNK, (c + 1) * CHUNK)
-            stage_chunk(c, first, count, bank, staged)
-            for u in range(count):
-                nc.vector.tensor_tensor(window(first + u, cols), staged[:, u, :], wgo_sb[:, cols], MULT)
+        def put_back(c, tiles, bank, staged):
+            cols = columns(c)
+            spans = stage([(n, cols) for n in tiles], bank, staged)
+            for n, span in zip(tiles, spans):
+                nc.vector.tensor_tensor(window(n, cols), staged[:, span], wgo_sb[:, cols], MULT)
 
         def weigh(values, cols):
             nc.gpsimd.tensor_tensor(values, values, wgo_sb[:, cols], MULT)
 
-        def stage_half(n, cols, bank, staged):
-            product(n, cols, flat(bank[:]))
-            nc.scalar.copy(staged, flat(bank[:]))
-            weigh(staged, cols)
-
         def scatter(n, cols, values):
             nc.vector.tensor_copy(window(n, cols), values)
 
-        def finish(engine, n, lo, hi):
+        def finish(engine, queue, n, lo, hi):
             engine.tensor_tensor(x0_sb[n][:, lo:hi], page[n][:, lo:hi], x0_sb[n][:, lo:hi], MULT)
-            nc.sync.dma_start(out[n * P : (n + 1) * P, lo:hi], x0_sb[n][:, lo:hi])
+            queue.dma_start(out[n * P : (n + 1) * P, lo:hi], x0_sb[n][:, lo:hi])
 
-        make_h(0)
-        prepare_w3(0)
-        make_z(0)
-        quantize_z(0)
-        for c in range(CHUNKS - 1):
-            make_h(c + 1)
-            put_back(c, 0, 1, banks_y[0], y[0])
+        make_h_fused(0, banks_y)
+        prepare_w3(0, tile("w3_grouped0", [P, PACK * W3_PIECE], BF16))
+        make_z(0, banks_y)
+        quantize_z(0, nc.vector.tensor_copy)
+        final = len(WIDTHS) - 1
+        for c in range(final):
+            if c + 1 < FUSED:
+                make_h_fused(c + 1, banks_a)
+            else:
+                make_h(c + 1)
             if c == 0:
-                prepare_w3(1)
-            make_z(c + 1)
-            put_back(c, 1, 2, banks_b[0], y[1])
-            quantize_z(c + 1)
-            put_back(c, 3, 1, banks_y[1], z)
-        prepare_w3(2)
+                prepare_w3(1, tile("w3_grouped1", [P, PACK * W3_PIECE], BF16))
+            put_back(c, [0], banks_y[0], y[0])
+            make_z(c + 1, banks_b)
+            put_back(c, [1, 2], banks_b[0], y[1])
+            quantize_z(c + 1, nc.vector.tensor_copy if c + 1 < VZB else nc.scalar.copy)
+            put_back(c, [3], banks_y[1], z)
+        prepare_w3(2, h_grouped)
 
         low, high = slice(0, S // 2), slice(S // 2, S)
-        last = slice(S - CHUNK, S)
-        spare = flat(z[:, 2:4, :])
-        product(4, low, flat(banks_y[2][:]))
-        nc.vector.tensor_tensor(spare, flat(banks_y[2][:]), wgo_sb[:, low], MULT)
+        last = columns(final)
+        spare = z[:, BANK : 2 * BANK]
+        third_product(4, low, banks_b[1][:])
+        nc.vector.tensor_tensor(spare, banks_b[1][:], wgo_sb[:, low], MULT)
         scatter(4, low, spare)
-        for i in range(2):
-            stage_chunk(CHUNKS - 1, PAIR * i, PAIR, banks_y[i], y[i])
-            for u in range(PAIR):
-                weigh(y[i][:, u, :], last)
-        stage_half(4, high, banks_y[3], flat(y[2][:]))
-        stage_half(5, low, banks_y[2], spare)
+        spans = [stage([(2 * i, last), (2 * i + 1, last)], banks_y[i], y[i]) for i in range(2)]
         for n in range(4):
-            scatter(n, last, y[n // PAIR][:, n % PAIR, :])
-            if n < 3:
-                finish(nc.gpsimd, n, 0, S)
-        stage_half(5, high, banks_b[1], flat(y[0][:]))
-        scatter(4, high, flat(y[2][:]))
-        finish(nc.gpsimd, 3, 0, S)
+            weigh(y[n // 2][:, spans[n // 2][n % 2]], last)
+        stage([(4, high)], banks_y[3], y[2])
+        weigh(y[2][:], high)
+        stage([(5, low)], banks_y[2], spare)
+        weigh(spare, low)
+        for n in range(4):
+            scatter(n, last, y[n // 2][:, spans[n // 2][n % 2]])
+            if n < 2:
+                finish(nc.gpsimd, nc.sync, n, 0, S)
+        stage([(5, high)], banks_b[1], y[0])
+        weigh(y[0][:], high)
+        scatter(4, high, y[2][:])
+        finish(nc.gpsimd, nc.sync, 2, 0, S)
+        finish(nc.gpsimd, nc.sync, 3, 0, S)
         scatter(5, low, spare)
-        finish(nc.gpsimd, 4, 0, S)
-        scatter(5, high, flat(y[0][:]))
-        finish(nc.vector, 5, 0, S // 2)
-        finish(nc.vector, 5, S // 2, S)
+        finish(nc.gpsimd, nc.sync, 4, 0, S)
+        scatter(5, high, y[0][:])
+        finish(nc.vector, nc.scalar, 5, 0, S // 2)
+        finish(nc.vector, nc.scalar, 5, S // 2, S)

@@ -337,7 +337,8 @@ def tile_list_jury_rank_cascade_kernel(
         finish(nc.gpsimd, nc.sync, 2, 0, S)
         finish(nc.gpsimd, nc.sync, 3, 0, S)
         scatter(5, low, spare)
-        finish(nc.gpsimd, nc.sync, 4, 0, S)
+        finish(nc.gpsimd, nc.sync, 4, 0, S // 2)
+        finish(nc.gpsimd, nc.sync, 4, S // 2, S)
         scatter(5, high, y[0][:])
         finish(nc.vector, nc.scalar, 5, 0, S // 2)
         finish(nc.vector, nc.scalar, 5, S // 2, S)

from contextlib import ExitStack

import concourse.mybir as mybir

K, H, N, T, S = 1024, 512, 768, 2048, 1024
FLOPS = 2 * S * (K * H + H * H + H * N)

F32 = mybir.dt.float32
BF16 = mybir.dt.bfloat16
I32 = mybir.dt.int32
U32 = mybir.dt.uint32
U16 = mybir.dt.uint16
U8 = mybir.dt.uint8
FP8X4 = mybir.dt.float8_e4m3fn_x4
FP4X4 = mybir.dt.float4_e2m1fn_x4
MULT = mybir.AluOpType.mult
ADD = mybir.AluOpType.add
ACT = mybir.ActivationFunctionType

P = 128
PACK = 4
BANK = 512
PER_COL = 16
PASSES = K // (P * PACK)
ROW_TILES = N // P
W3_PIECE = 256
WIDTHS = (256, 256, 256, 256)
WIDE = 256
FUSED = 2
VZB = 1
VW3 = 2


def tile_list_jury_rank_cascade_kernel(
    tc, tab_words, tab_scales, offs, offs2, w1, ga, w2_words, w2_scales, gb, w3, wgo, x0, out
):
    nc = tc.nc
    with ExitStack() as ctx:
        keep = ctx.enter_context(tc.tile_pool(name="keep", bufs=1))
        psum = ctx.enter_context(tc.psum_pool(name="psum", bufs=1))

        def tile(name, shape, dtype):
            return keep.tile(shape, dtype, name=name, align_bytes=64)

        picks = keep.tile([P, S // PER_COL], U16, name="picks")
        places = keep.tile([P, S // PER_COL], U16, name="places")
        table = [tile("table%d" % a, [P, T], I32) for a in range(PASSES)]
        table_scale = tile("table_scale", [P, T], U8)
        w1_early = tile("w1_early", [P, PACK, H], F32)
        w1_late = [tile("w1_late%d" % i, [P, PACK, H // 2], F32) for i in range(2)]
        w3_raw = [tile("w3_raw%d" % i, [P, PACK, W3_PIECE], F32) for i in range(N // W3_PIECE)]
        wgo_sb = tile("wgo_sb", [P, S], F32)
        x0_sb = [tile("x0_sb%d" % n, [P, S], F32) for n in range(ROW_TILES)]
        w2_raw = tile("w2_raw", [P, 2 * H], U8)
        w2_raw_scale = tile("w2_raw_scale", [P, H], U8)
        ga_sb = tile("ga_sb", [P, PACK], F32)
        gb_sb = tile("gb_sb", [P, PACK], F32)

        nc.gpsimd.memset(table_scale[:].bitcast(I32), 0)
        zero_in = tile("zero_in", [P, 1], F32)
        zero = tile("zero", [P, 1], F32)
        nc.vector.memset(zero_in[:], 0.0)
        nc.scalar.activation(zero[:], zero_in[:], ACT.Gelu_apprx_tanh)

        def load_table(a):
            nc.sync.dma_start(table[a][:], tab_words[a].rearrange("p t i -> p (t i)").bitcast(I32))

        def load_w1(raw, a, cols):
            rows = w1[a * P * PACK : (a + 1) * P * PACK, cols]
            nc.sync.dma_start(raw[:], rows.rearrange("(p j) c -> p j c", j=PACK))

        def load_w3(i):
            cols = w3[:, i * W3_PIECE : (i + 1) * W3_PIECE]
            nc.sync.dma_start(w3_raw[i][:], cols.rearrange("(p j) c -> p j c", j=PACK))

        nc.gpsimd.memset(w2_raw_scale[:].bitcast(I32), 0)
        nc.gpsimd.dma_start(ga_sb[:], ga.rearrange("(p t) -> p t", t=PACK))
        nc.gpsimd.dma_start(gb_sb[:], gb.rearrange("(p t) -> p t", t=PACK))

        nc.sync.dma_start(picks[:], offs)
        nc.sync.dma_start(w2_raw[:].bitcast(I32), w2_words[0].bitcast(I32))
        nc.sync.dma_start(places[:], offs2)
        for q in range(4):
            nc.sync.dma_start(
                table_scale[32 * q : 32 * q + 4 * PASSES, :].bitcast(I32),
                tab_scales.bitcast(I32)[:, 4 * q : 4 * q + 4, :],
            )
        load_table(0)
        load_table(1)
        load_w1(w1_early, 0, slice(0, H))
        for q in range(4):
            nc.sync.dma_start(
                w2_raw_scale[32 * q : 32 * q + 4, :].bitcast(I32),
                w2_scales[0].bitcast(I32)[4 * q : 4 * q + 4, :],
            )
        for i in range(2):
            load_w1(w1_late[i], 1, slice(i * H // 2, (i + 1) * H // 2))
        load_w3(0)
        nc.sync.dma_start(wgo_sb[:], wgo)
        load_w3(1)
        load_w3(2)
        for n in range(ROW_TILES):
            nc.sync.dma_start(x0_sb[n][:], x0[n * P : (n + 1) * P, :])

        picked = [tile("picked%d" % a, [P, S], U32) for a in range(PASSES)]
        picked_scale = tile("picked_scale", [P, S], U8)

        nc.vector.tensor_copy(picked_scale[:], table_scale[:].indirect(picks[:]))
        for a in range(PASSES):
            nc.vector.tensor_copy(picked[a][:], table[a][:].bitcast(U32).indirect(picks[:]))

        def quantize(codes, scale, grouped):
            nc.vector.quantize_mx(out=codes.bitcast(FP8X4), scales=scale, in_=grouped)

        w1_codes = [tile("w1_codes%d" % a, [P, H], U32) for a in range(PASSES)]
        w1_scale = [tile("w1_scale%d" % a, [P, H], U8) for a in range(PASSES)]
        w1_grouped = [tile("w1_grouped%d" % a, [P, PACK * H], BF16) for a in range(PASSES)]

        def group_w1(copy, a, half, raw):
            dst = w1_grouped[a][:].rearrange("p (t m j) -> p m j t", t=PACK, j=PACK)
            copy(dst[:, half * P // 2 : (half + 1) * P // 2], raw.rearrange("p j (m t) -> p m j t", t=PACK))

        group_w1(nc.scalar.copy, 0, 0, w1_early[:, :, 0 : H // 2])
        group_w1(nc.vector.tensor_copy, 0, 1, w1_early[:, :, H // 2 : H])
        quantize(w1_codes[0][:], w1_scale[0][:], w1_grouped[0][:])
        group_w1(nc.scalar.copy, 1, 0, w1_late[0][:])
        group_w1(nc.vector.tensor_copy, 1, 1, w1_late[1][:])
        for lo in (0, H // 2):
            cols = slice(lo, lo + H // 2)
            quantize(w1_codes[1][:, cols], w1_scale[1][:, cols], w1_grouped[1][:, PACK * cols.start : PACK * cols.stop])

        w2_codes = tile("w2_codes", [P, 2 * H], U8)
        w2_scale = tile("w2_scale", [P, H], U8)
        nc.vector.tensor_copy(
            w2_codes[:].bitcast(U16).rearrange("p (t m) -> p t m", t=PACK),
            w2_raw[:].bitcast(U16).rearrange("p (m t) -> p t m", t=PACK),
        )
        nc.vector.tensor_copy(
            w2_scale[:].rearrange("p (t m) -> p t m", t=PACK),
            w2_raw_scale[:].rearrange("p (m t) -> p t m", t=PACK),
        )

        def interleave(copy, grouped, planes):
            copy(
                grouped.rearrange("p (c i t) -> p c t i", i=4, t=PACK),
                planes.rearrange("p t (c i) -> p c t i", i=4),
            )

        w3_codes = tile("w3_codes", [P, N], U32)
        w3_scale = tile("w3_scale", [P, N], U8)

        def prepare_w3(i, grouped):
            interleave(nc.vector.tensor_copy if i < VW3 else nc.scalar.copy, grouped[:], w3_raw[i][:])
            cols = slice(i * W3_PIECE, (i + 1) * W3_PIECE)
            quantize(w3_codes[:, cols], w3_scale[:, cols], grouped[:])

        banks = [psum.tile([P, BANK], F32, name="bank%d" % i) for i in range(8)]
        banks_a, banks_b, banks_y = banks[0:2], banks[2:4], banks[4:8]

        gelus = [tile("gelu%d" % i, [P, PACK * WIDE], F32) for i in range(2)]
        h = [tile("h%d" % i, [P, PACK * WIDE], F32) for i in range(2)]
        h_grouped = tile("h_grouped", [P, PACK * WIDE], BF16)
        h_codes = tile("h_codes", [P, WIDE], U32)
        h_scale = tile("h_scale", [P, WIDE], U8)
        bent = tile("bent", [P, PACK * WIDE], F32)
        z = tile("z", [P, PACK * WIDE], F32)
        z_grouped = tile("z_grouped", [P, PACK * WIDE], BF16)
        z_codes = tile("z_codes", [P, S], U32)
        z_scale = tile("z_scale", [P, S], U8)
        y = [tile("y%d" % i, [P, BANK], F32) for i in range(3)]
        page = [tile("page%d" % n, [P, S], F32) for n in range(ROW_TILES)]

        def columns(c):
            return slice(sum(WIDTHS[:c]), sum(WIDTHS[: c + 1]))

        def planes(flat, width):
            return flat[:, 0 : PACK * width].rearrange("p (t c) -> p t c", t=PACK)

        def first_product(c, t, acc):
            cols = columns(c)
            ch = slice(t * P, (t + 1) * P)
            for a in range(PASSES):
                nc.tensor.matmul_mx(
                    out=acc,
                    lhsT=w1_codes[a][:, ch].bitcast(FP8X4),
                    lhsT_scale=w1_scale[a][:, ch],
                    rhs=picked[a][:, cols].bitcast(FP8X4),
                    rhs_scale=picked_scale[4 * a : P, cols],
                    start=(a == 0),
                    stop=(a == PASSES - 1),
                )

        def second_product(c, t, acc):
            width = WIDTHS[c]
            nc.tensor.matmul_mx(
                out=acc,
                lhsT=w2_codes[:, 2 * t * P : 2 * (t + 1) * P].bitcast(FP4X4),
                lhsT_scale=w2_scale[:, t * P : (t + 1) * P],
                rhs=h_codes[:, 0:width].bitcast(FP8X4),
                rhs_scale=h_scale[:, 0:width],
                start=True,
                stop=True,
            )

        def activate(c, product, func, dst, used, after):
            width = WIDTHS[c]
            share = PACK // len(used)
            for i, bank in enumerate(used):
                for u in range(share):
                    product(c, share * i + u, bank[:, u * width : (u + 1) * width])
                span = slice(share * i * width, share * (i + 1) * width)
                nc.scalar.activation(dst[:, span], bank[:, 0 : share * width], func, bias=zero[:])
                for t in range(share * i, share * (i + 1)):
                    after(t, slice(t * width, (t + 1) * width))

        def quantize_h(c):
            width = WIDTHS[c]
            quantize(h_codes[:, 0:width], h_scale[:, 0:width], h_grouped[:, 0 : PACK * width])

        def gain(c, t, plane):
            nc.scalar.activation(h[c % 2][:, plane], gelus[min(c, 1)][:, plane], ACT.Copy, scale=ga_sb[:, t : t + 1])

        def make_h_fused(c, used):
            width = WIDTHS[c]
            activate(c, first_product, ACT.Gelu_apprx_tanh, gelus[min(c, 1)], used, lambda t, plane: None)
            gains = ga_sb[:].unsqueeze(1).unsqueeze(3).to_broadcast([P, width // 4, PACK, 4])
            nc.vector.tensor_tensor(
                h_grouped[:, 0 : PACK * width].rearrange("p (c i t) -> p c t i", i=4, t=PACK),
                planes(gelus[min(c, 1)], width).rearrange("p t (c i) -> p c t i", i=4),
                gains,
                MULT,
            )
            quantize_h(c)
            for t in range(PACK):
                gain(c, t, slice(t * width, (t + 1) * width))

        def make_h(c):
            width = WIDTHS[c]
            activate(c, first_product, ACT.Gelu_apprx_tanh, gelus[min(c, 1)], banks_a, lambda t, plane: gain(c, t, plane))
            interleave(nc.scalar.copy, h_grouped[:, 0 : PACK * width], planes(h[c % 2], width))
            quantize_h(c)

        def make_z(c, used):
            def add(t, plane):
                nc.vector.scalar_tensor_tensor(
                    z[:, plane], bent[:, plane], gb_sb[:, t : t + 1], h[c % 2][:, plane], MULT, ADD
                )

            activate(c, second_product, ACT.Tanh, bent, used, add)

        def quantize_z(c, copy):
            width = WIDTHS[c]
            cols = columns(c)
            interleave(copy, z_grouped[:, 0 : PACK * width], planes(z, width))
            quantize(z_codes[:, cols], z_scale[:, cols], z_grouped[:, 0 : PACK * width])

        def third_product(n, cols, acc):
            rows = slice(n * P, (n + 1) * P)
            nc.tensor.matmul_mx(
                out=acc,
                lhsT=w3_codes[:, rows].bitcast(FP8X4),
                lhsT_scale=w3_scale[:, rows],
                rhs=z_codes[:, cols].bitcast(FP8X4),
                rhs_scale=z_scale[:, cols],
                start=True,
                stop=True,
            )

        def window(n, cols):
            return page[n][:].indirect(places[:, cols.start // PER_COL : cols.stop // PER_COL])

        def stage(pieces, bank, staged):
            spans = []
            used = 0
            for n, cols in pieces:
                spans.append(slice(used, used + cols.stop - cols.start))
                third_product(n, cols, bank[:, spans[-1]])
                used = spans[-1].stop
            nc.scalar.copy(staged[:, 0:used], bank[:, 0:used])
            return spans

        def put_back(c, tiles, bank, staged):
            cols = columns(c)
            spans = stage([(n, cols) for n in tiles], bank, staged)
            for n, span in zip(tiles, spans):
                nc.vector.tensor_tensor(window(n, cols), staged[:, span], wgo_sb[:, cols], MULT)

        def weigh(values, cols):
            nc.gpsimd.tensor_tensor(values, values, wgo_sb[:, cols], MULT)

        def scatter(n, cols, values):
            nc.vector.tensor_copy(window(n, cols), values)

        def finish(engine, queue, n, lo, hi):
            engine.tensor_tensor(x0_sb[n][:, lo:hi], page[n][:, lo:hi], x0_sb[n][:, lo:hi], MULT)
            queue.dma_start(out[n * P : (n + 1) * P, lo:hi], x0_sb[n][:, lo:hi])

        make_h_fused(0, banks_y)
        prepare_w3(0, tile("w3_grouped0", [P, PACK * W3_PIECE], BF16))
        make_z(0, banks_y)
        quantize_z(0, nc.vector.tensor_copy)
        final = len(WIDTHS) - 1
        for c in range(final):
            if c + 1 < FUSED:
                make_h_fused(c + 1, banks_a)
            else:
                make_h(c + 1)
            if c == 0:
                prepare_w3(1, tile("w3_grouped1", [P, PACK * W3_PIECE], BF16))
            put_back(c, [0], banks_y[0], y[0])
            make_z(c + 1, banks_b)
            put_back(c, [1, 2], banks_b[0], y[1])
            quantize_z(c + 1, nc.vector.tensor_copy if c + 1 < VZB else nc.scalar.copy)
            put_back(c, [3], banks_y[1], z)
        prepare_w3(2, h_grouped)

        low, high = slice(0, S // 2), slice(S // 2, S)
        last = columns(final)
        spare = z[:, BANK : 2 * BANK]
        third_product(4, low, banks_b[1][:])
        nc.vector.tensor_tensor(spare, banks_b[1][:], wgo_sb[:, low], MULT)
        scatter(4, low, spare)
        spans = [stage([(2 * i, last), (2 * i + 1, last)], banks_y[i], y[i]) for i in range(2)]
        for n in range(4):
            weigh(y[n // 2][:, spans[n // 2][n % 2]], last)
        stage([(4, high)], banks_y[3], y[2])
        weigh(y[2][:], high)
        stage([(5, low)], banks_y[2], spare)
        weigh(spare, low)
        for n in range(4):
            scatter(n, last, y[n // 2][:, spans[n // 2][n % 2]])
            if n < 2:
                finish(nc.gpsimd, nc.sync, n, 0, S)
        stage([(5, high)], banks_b[1], y[0])
        weigh(y[0][:], high)
        scatter(4, high, y[2][:])
        finish(nc.gpsimd, nc.sync, 2, 0, S)
        finish(nc.gpsimd, nc.sync, 3, 0, S)
        scatter(5, low, spare)
        finish(nc.gpsimd, nc.sync, 4, 0, S // 2)
        finish(nc.gpsimd, nc.sync, 4, S // 2, S)
        scatter(5, high, y[0][:])
        finish(nc.vector, nc.scalar, 5, 0, S // 2)
        finish(nc.vector, nc.scalar, 5, S // 2, S)
